import numpy as np, ml_dtypes
CORES = [21,109,149,237,277,365,405,493,150,406]
N = 10
import mx_ref
NC, W = 128, 6
BF = ml_dtypes.bfloat16
def cut(t, i, w=512):
    return t[:, w * i:w * i + w]
def term(a, B):
    return np.stack([mx_ref.matmul(mx_ref.quantize(cut(a, i)), B) for i in range(4)], axis=2).reshape(128, -1)
def setup_inputs(rng):
    def f(*shape):
        return mx_ref.flush((rng.standard_normal(shape, dtype=np.float32) * np.exp2(rng.integers(-2, 3, shape[:-1] + (1,)))).astype(BF))
    return {"a": f(N, 128, 4 * 512), "b": f(N, 128, 4 * NC)}
def setup_inputs_blocks(rng):
    d = setup_inputs(rng)
    for k in ("a", "b"): d[k] = mx_ref.spread(d[k], rng, 2)
    return d
def setup_inputs_wide(rng):
    d = setup_inputs(rng)
    for k in ("a", "b"): d[k] = mx_ref.flush((d[k].astype(np.float32) * np.exp2(rng.integers(-4, 5, (N, 1, 1))).astype(np.float32)).astype(BF))
    return d
def setup_inputs_lossless(rng):
    a = np.zeros((N, 128, 4 * 128, 4), np.float32)
    for r in range(N):
        k = rng.integers(0, 512, size=4 * 128)
        a[r, k // 4, np.arange(4 * 128), k % 4] = 1.0
    size = np.repeat(2.0 ** rng.integers(-4, 5, size=(1, 1, (4 * NC) // 4)), 4, axis=2)
    b = rng.integers(-1, 2, size=(N, 128, 4 * NC)) * size
    return {"a": a.reshape(N, 128, 4 * 512).astype(BF), "b": b.astype(np.float32).astype(BF)}
def reference(a, b):
    T = [term(a[r], mx_ref.quantize(b[r])) for r in range(N)]
    y = np.zeros((N, 128, 4 * NC), np.float32)
    for c in range(N):
        y[c] = mx_ref.total([T[(c - k) % N] for k in range(W)])
    return {"y": y}

@@ -1,0 +1,195 @@
+from concourse.mybir import dt, AluOpType, ActivationFunctionType
+
+BF, F8, U8, F32 = "bfloat16", "float8_e4m3fn_x4", "uint8", "float32"
+SCRATCH = {
+    "a_sb": ("sbuf", [128, 2048], BF), "b_sb": ("sbuf", [128, 512], BF),
+    "aq": ("sbuf", [128, 512], F8), "aqs": ("sbuf", [128, 512], U8),
+    "bq": ("sbuf", [128, 128], F8), "bqs": ("sbuf", [128, 128], U8),
+    "ones": ("sbuf", [128, 516], BF), "sel": ("sbuf", [128, 516], BF),
+    "w": ("sbuf", [128, 512], F8), "ws": ("sbuf", [128, 512], U8),
+    "h0": ("sbuf", [128, 512], BF), "q0": ("sbuf", [128, 128], F8), "s0": ("sbuf", [128, 128], U8),
+    "h1": ("sbuf", [128, 512], BF), "q1": ("sbuf", [128, 128], F8), "s1": ("sbuf", [128, 128], U8),
+    "l0": ("sbuf", [128, 128], F8), "m0": ("sbuf", [128, 128], U8),
+    "l1": ("sbuf", [128, 128], F8), "m1": ("sbuf", [128, 128], U8),
+    "l2": ("sbuf", [128, 128], F8), "m2": ("sbuf", [128, 128], U8),
+    "y_sb": ("sbuf", [128, 512], F32),
+    "p0": ("psum", [128, 2048], F32), "p1": ("psum", [128, 2048], F32),
+}
+SEMAPHORES = (["ldb", "ld0", "ld1", "ld2", "ld3", "qb", "qa0", "qa1", "qa2", "qa3", "one", "sl", "cq",
+               "cp0", "cp1", "qz0", "qz1", "arr0", "arr1", "arr2", "sent", "stored"]
+              + ["pe%d_%d" % (s, b) for s in range(2) for b in range(4)])
+
+OWN, MATE, NEAR, FAR = 0, 1, 0, 1
+RELAYS = {
+    "A": (0, OWN, FAR), "B": (1, OWN, NEAR), "C": (2, OWN, NEAR), "D": (3, OWN, NEAR), "E": (4, OWN, NEAR),
+    "F": (5, MATE, NEAR), "G": (5, OWN, FAR), "H": (5, OWN, NEAR), "I": (6, OWN, NEAR), "J": (6, MATE, FAR),
+    "K": (7, OWN, FAR),
+}
+SEND = {
+    0: [((0,), "A", 1), ((0,), "C", 0)],
+    1: [((1,), "D", 0), ((1,), "K", 0)],
+    2: [((2,), "F", 0), ((2,), "C", 1)],
+    3: [((3,), "H", 0), ((3,), "G", 0), ((3,), 5, 0)],
+    4: [((4,), "C", 0), ((4,), "F", 0), ((4,), "I", 0)],
+    5: [((5,), "G", 0), ((5,), "J", 0), ((5,), "K", 0)],
+    6: [((6,), "I", 0), ((6,), "E", 0), ((6,), "F", 0)],
+    7: [((7,), "B", 0), ((7,), "J", 0), ((7,), "G", 0)],
+    8: [((8,), "D", 0), ((8,), "B", 0), ((8,), 0, 0)],
+    9: [((9,), "A", 0), ((9,), "I", 0), ((9,), "H", 0), ((9,), "B", 0)],
+    "A": [((0,), 1, 0), ((0, 9), 3, 0), ((0, 9), 2, 0)],
+    "B": [((7,), 2, 0), ((7, 8), 9, 0), ((7, 8, 9), 1, 0)],
+    "C": [((4,), 8, 0), ((2, 0), 4, 0), ((4, 2, 0), 5, 0)],
+    "D": [((1,), 5, 0), ((1, 8), 3, 0), ((1, 8), 2, 0)],
+    "E": [((6,), 8, 0)],
+    "F": [((2,), 3, 0), ((2, 4), 6, 0), ((2, 4, 6), 7, 0)],
+    "G": [((5,), 9, 0), ((5, 3), 7, 0), ((5, 3, 7), 8, 0)],
+    "H": [((3,), 6, 0), ((3, 9), 4, 0)],
+    "I": [((6,), 1, 0), ((6, 9), 0, 0), ((6, 4), 9, 1)],
+    "J": [((5, 7), 0, 0)],
+    "K": [((1,), 4, 0), ((1, 5), 6, 0)],
+}
+FINAL = {
+    0: [(8,), (6, 9), (5, 7)], 1: [(0,), (6,), (7, 8, 9)], 2: [(7,), (0, 9), (1, 8)], 3: [(2,), (0, 9), (1, 8)],
+    4: [(2, 0), (1,), (3, 9)], 5: [(3,), (1,), (4, 2, 0)], 6: [(3,), (2, 4), (1, 5)], 7: [(5, 3), (2, 4, 6)],
+    8: [(4,), (6,), (5, 3, 7)], 9: [(5,), (7, 8), (6, 4)],
+}
+WORLD = 512
+PLACES = {}
+
+
+def place(T, topo):
+    if PLACES:
+        return PLACES
+    PLACES.update({r: c for r, c in enumerate(T.cores)})
+    for name in sorted(RELAYS):
+        anchor, mate, far = RELAYS[name]
+        a = T.cores[anchor]
+        for c in range(WORLD):
+            here = topo.mates(c, a) if mate else (topo.host(c), topo.chip(c)) == (topo.host(a), topo.chip(a))
+            if not here or (topo.die(c) != topo.die(a)) != bool(far) or c in PLACES.values():
+                continue
+            if any(topo.mates(c, d) and topo.may_write(c, d) for d in range(WORLD)):
+                PLACES[name] = c
+                break
+    return PLACES
+
+
+def rank_program(g, core, T, topo):
+    at = place(T, topo)
+    names = [n for n in at if at[n] == core]
+    if not names:
+        return
+    me = names[0]
+    rank = T.rank_of(core)
+    sem = T.sem
+    slots = {n: [] for n in at}
+    for n in SEND:
+        for terms, d, _ in SEND[n]:
+            slots[d].append((n, terms))
+    slot_of = {terms: k for k, (n, terms) in enumerate(slots[me])}
+
+    def landed(k):
+        return T["l%d" % k], T["m%d" % k]
+
+    def unpack(ps, k, start, stop, stage):
+        codes, plane = landed(k)
+        g.tensor.wait_ge(sem["arr%d" % k], 16)
+        for b in (0, 2, 1, 3):
+            i = g.tensor.matmul_mx(ps[:, 512 * b:512 * b + 128], T.w[:, 128 * b:128 * b + 128],
+                                   T.ws[:, 128 * b:128 * b + 128], codes[:], plane[:], start, stop)
+            if stop:
+                i.then_inc(sem["pe%d_%d" % (stage, b)], 1)
+
+    def empty(ps, out, stage, vec, act):
+        for b in vec:
+            g.vector.wait_ge(sem["pe%d_%d" % (stage, b)], 1)
+            g.vector.tensor_copy(out[:, b:512:4], ps[:, 512 * b:512 * b + 128]).then_inc(sem["cp%d" % stage], 1)
+        for b in act:
+            g.scalar.wait_ge(sem["pe%d_%d" % (stage, b)], 1)
+            g.scalar.activation(out[:, b:512:4], ps[:, 512 * b:512 * b + 128],
+                                ActivationFunctionType.Copy).then_inc(sem["cp%d" % stage], 1)
+
+    def pack(stage):
+        g.vector.wait_ge(sem["cp%d" % stage], 4)
+        g.vector.quantize_mx(T["q%d" % stage][:], T["s%d" % stage][:], T["h%d" % stage][:]).then_inc(sem["qz%d" % stage], 1)
+
+    def selections():
+        g.vector.wait_ge(sem.sl, 1)
+        for b in range(4):
+            g.vector.quantize_mx(T.w[:, 128 * b:128 * b + 128], T.ws[:, 128 * b:128 * b + 128],
+                                 T.sel[:, 3 - b:515 - b]).then_inc(sem.cq, 1)
+
+    if rank is not None or any(len(terms) > 1 for terms, d, _ in SEND[me]):
+        g.vector.memset(T.ones[:], 1.0).then_inc(sem.one, 1)
+        g.wait_ge(sem.one, 1)
+        g.affine_select(T.sel[:], T.ones[:], [[-1, 516]], AluOpType.is_equal, 0.0, 3, 4).then_inc(sem.sl, 1)
+
+    ready = {}
+    if rank is not None:
+        def piece(i):
+            return slice(512 * i, 512 * i + 512)
+        g.sync.dma_start(T.b_sb[:], T.b[:]).then_inc(sem.ldb, 16)
+        for i, q in ((0, g.scalar), (1, g.sync), (2, g.scalar), (3, g.sync)):
+            q.dma_start(T.a_sb[:, piece(i)], T.a[:, piece(i)]).then_inc(sem["ld%d" % i], 16)
+        g.vector.wait_ge(sem.ldb, 16)
+        g.vector.quantize_mx(T.bq[:], T.bqs[:], T.b_sb[:]).then_inc(sem.qb, 1)
+        for i in range(4):
+            g.vector.wait_ge(sem["ld%d" % i], 16)
+            g.vector.quantize_mx(T.aq[:, 128 * i:128 * i + 128], T.aqs[:, 128 * i:128 * i + 128],
+                                 T.a_sb[:, piece(i)]).then_inc(sem["qa%d" % i], 1)
+        g.tensor.wait_ge(sem.qb, 1)
+
+        def product(ps, i, stop):
+            return g.tensor.matmul_mx(ps[:, 512 * i:512 * i + 128], T.aq[:, 128 * i:128 * i + 128],
+                                      T.aqs[:, 128 * i:128 * i + 128], T.bq[:], T.bqs[:], True, stop)
+        for i in range(4):
+            g.tensor.wait_ge(sem["qa%d" % i], 1)
+            product(T.p0, i, True).then_inc(sem["pe0_%d" % i], 1)
+        empty(T.p0, T.h0, 0, (3,), (0, 1, 2))
+        pack(0)
+        ready[(rank,)] = (sem.qz0, 1, T.q0, T.s0)
+        selections()
+        for i in range(4):
+            product(T.p1, i, False)
+        g.tensor.wait_ge(sem.cq, 4)
+        for n, terms in enumerate(FINAL[rank]):
+            unpack(T.p1, slot_of[terms], False, n == len(FINAL[rank]) - 1, 1)
+        empty(T.p1, T.y_sb, 1, (0, 1), (2, 3))
+        g.sync.wait_ge(sem.cp1, 4)
+        g.sync.dma_start(T.y[:], T.y_sb[:]).then_inc(sem.stored, 16)
+        g.sync.wait_ge(sem.stored, 16)
+    else:
+        sums = []
+        for terms, d, _ in SEND[me]:
+            if len(terms) == 1:
+                k = slot_of[terms]
+                ready[terms] = (sem["arr%d" % k], 16) + landed(k)
+            elif terms not in sums:
+                sums.append(terms)
+        if sums:
+            selections()
+            g.tensor.wait_ge(sem.cq, 4)
+        for stage, terms in enumerate(sums):
+            ps = T["p%d" % stage]
+            for n, r in enumerate(terms):
+                unpack(ps, slot_of[(r,)], n == 0, n == len(terms) - 1, stage)
+            empty(ps, T["h%d" % stage], stage, (0, 1), (2, 3))
+            pack(stage)
+            ready[terms] = (sem["qz%d" % stage], 1, T["q%d" % stage], T["s%d" % stage])
+
+    away = next(c for c in range(WORLD) if (topo.host(c), topo.chip(c)) != (topo.host(core), topo.chip(core))
+                and topo.may_write(core, c))
+    off = topo.mask(core, away)
+    signals = 0
+    for terms, d, beside in SEND[me]:
+        s, v, codes, plane = ready[terms]
+        g.wait_ge(s, v)
+        dst = at[d]
+        k = slots[d].index((me, terms))
+        rid, pid = topo.addr(dst, core)
+        mask = topo.mask(core, dst) & (~off if beside else off)
+        cl, pl = landed(k)
+        g.remote_dma(cl[:].bitcast(dt.uint8), codes[:].bitcast(dt.uint8), sem["arr%d" % k], sem.sent, pid, rid, mask)
+        g.remote_dma(pl[:], plane[:], sem["arr%d" % k], sem.sent, pid, rid, mask)
+        signals += 2 * bin(mask).count("1")
+    g.wait_ge(sem.sent, signals)

@@ -15,43 +15,45 @@ SCRATCH = {
     "y_sb": ("sbuf", [128, 512], F32),
     "p0": ("psum", [128, 2048], F32), "p1": ("psum", [128, 2048], F32),
 }
-SEMAPHORES = (["ldb", "ld0", "ld1", "ld2", "ld3", "qb", "qa0", "qa1", "qa2", "qa3", "one", "sl", "cq",
-               "cp0", "cp1", "qz0", "qz1", "arr0", "arr1", "arr2", "sent", "stored"]
-              + ["pe%d_%d" % (s, b) for s in range(2) for b in range(4)])
+SEMAPHORES = (["ldb", "lda", "ldz", "qb", "qa0", "qa1", "qa2", "qa3", "one", "sl", "cq",
+               "cp0", "cp1", "cp2", "qz0", "qz1", "arr0", "arr1", "arr2", "sent", "stored"]
+              + ["pe%d_%d" % (s, b) for s in range(3) for b in range(4)])
 
 OWN, MATE, NEAR, FAR = 0, 1, 0, 1
 RELAYS = {
-    "A": (0, OWN, FAR), "B": (1, OWN, NEAR), "C": (2, OWN, NEAR), "D": (3, OWN, NEAR), "E": (4, OWN, NEAR),
-    "F": (5, MATE, NEAR), "G": (5, OWN, FAR), "H": (5, OWN, NEAR), "I": (6, OWN, NEAR), "J": (6, MATE, FAR),
-    "K": (7, OWN, FAR),
+    "A": (0, OWN, NEAR), "B": (1, OWN, NEAR), "C": (1, OWN, FAR), "D": (2, OWN, FAR), "E": (2, OWN, NEAR),
+    "F": (2, MATE, NEAR), "G": (3, OWN, NEAR), "H": (4, OWN, NEAR), "I": (5, OWN, NEAR), "J": (5, OWN, NEAR),
+    "K": (5, MATE, NEAR), "L": (6, OWN, NEAR), "M": (0, MATE, FAR),
 }
 SEND = {
-    0: [((0,), "A", 1), ((0,), "C", 0)],
-    1: [((1,), "D", 0), ((1,), "K", 0)],
-    2: [((2,), "F", 0), ((2,), "C", 1)],
-    3: [((3,), "H", 0), ((3,), "G", 0), ((3,), 5, 0)],
-    4: [((4,), "C", 0), ((4,), "F", 0), ((4,), "I", 0)],
-    5: [((5,), "G", 0), ((5,), "J", 0), ((5,), "K", 0)],
-    6: [((6,), "I", 0), ((6,), "E", 0), ((6,), "F", 0)],
-    7: [((7,), "B", 0), ((7,), "J", 0), ((7,), "G", 0)],
-    8: [((8,), "D", 0), ((8,), "B", 0), ((8,), 0, 0)],
-    9: [((9,), "A", 0), ((9,), "I", 0), ((9,), "H", 0), ((9,), "B", 0)],
-    "A": [((0,), 1, 0), ((0, 9), 3, 0), ((0, 9), 2, 0)],
-    "B": [((7,), 2, 0), ((7, 8), 9, 0), ((7, 8, 9), 1, 0)],
-    "C": [((4,), 8, 0), ((2, 0), 4, 0), ((4, 2, 0), 5, 0)],
-    "D": [((1,), 5, 0), ((1, 8), 3, 0), ((1, 8), 2, 0)],
-    "E": [((6,), 8, 0)],
-    "F": [((2,), 3, 0), ((2, 4), 6, 0), ((2, 4, 6), 7, 0)],
-    "G": [((5,), 9, 0), ((5, 3), 7, 0), ((5, 3, 7), 8, 0)],
-    "H": [((3,), 6, 0), ((3, 9), 4, 0)],
-    "I": [((6,), 1, 0), ((6, 9), 0, 0), ((6, 4), 9, 1)],
-    "J": [((5, 7), 0, 0)],
-    "K": [((1,), 4, 0), ((1, 5), 6, 0)],
+    0: [((0,), "D", 0), ((0,), "E", 0), ((0,), 2, 0)],
+    1: [((1,), "C", 0), ((1,), "F", 0), ((1,), 3, 0), ((1,), "B", 1)],
+    2: [((2,), "K", 0), ((2,), "E", 1), ((2,), "H", 0), ((2, 0), 4, 0)],
+    3: [((3,), "I", 0), ((3,), "G", 1), ((3,), "J", 0), ((3, 1), 5, 0)],
+    4: [((4,), "H", 1), ((4,), "L", 0), ((4,), "D", 0)],
+    5: [((5,), "I", 0), ((5,), "G", 0), ((5,), "F", 0)],
+    6: [((6,), "H", 0), ((6,), "A", 0), ((6,), "L", 1), ((6,), "K", 0)],
+    7: [((7,), "B", 0), ((7,), "M", 0), ((7,), "C", 0)],
+    8: [((8,), "E", 0), ((8,), "B", 0), ((8,), "A", 0)],
+    9: [((9,), "A", 0), ((9,), "J", 0)],
+    "A": [((9,), 2, 0), ((9, 6, 8), 0, 1), ((9, 6, 8), 1, 0)],
+    "B": [((7,), 1, 0), ((7, 8), 9, 0), ((7, 8, 1), 2, 0)],
+    "C": [((1,), 6, 0), ((7,), 0, 0)],
+    "D": [((0,), 1, 0), ((0, 4), 5, 0)],
+    "E": [((8, 2, 0), 3, 0)],
+    "F": [((1,), 4, 0), ((5,), 0, 0)],
+    "G": [((3, 5), 8, 0)],
+    "H": [((4,), 7, 0), ((4, 6), 8, 0), ((4, 2), 6, 0)],
+    "I": [((5,), 9, 0), ((5, 3), 6, 0), ((5, 3), 7, 0)],
+    "J": [((9,), 3, 0), ((9, 3), 4, 0)],
+    "K": [((2,), 5, 0), ((2, 6), 7, 0)],
+    "L": [((6, 4), 9, 0)],
+    "M": [((7,), 8, 0)],
 }
 FINAL = {
-    0: [(8,), (6, 9), (5, 7)], 1: [(0,), (6,), (7, 8, 9)], 2: [(7,), (0, 9), (1, 8)], 3: [(2,), (0, 9), (1, 8)],
-    4: [(2, 0), (1,), (3, 9)], 5: [(3,), (1,), (4, 2, 0)], 6: [(3,), (2, 4), (1, 5)], 7: [(5, 3), (2, 4, 6)],
-    8: [(4,), (6,), (5, 3, 7)], 9: [(5,), (7, 8), (6, 4)],
+    0: [(9, 6, 8), (7,), (5,)], 1: [(7,), (0,), (9, 6, 8)], 2: [(0,), (9,), (7, 8, 1)], 3: [(1,), (9,), (8, 2, 0)],
+    4: [(1,), (2, 0), (9, 3)], 5: [(2,), (3, 1), (0, 4)], 6: [(1,), (5, 3), (4, 2)], 7: [(4,), (5, 3), (2, 6)],
+    8: [(4, 6), (3, 5), (7,)], 9: [(5,), (7, 8), (6, 4)],
 }
 WORLD = 512
 PLACES = {}
@@ -112,6 +114,7 @@ def rank_program(g, core, T, topo):
     def pack(stage):
         g.vector.wait_ge(sem["cp%d" % stage], 4)
         g.vector.quantize_mx(T["q%d" % stage][:], T["s%d" % stage][:], T["h%d" % stage][:]).then_inc(sem["qz%d" % stage], 1)
+        return sem["qz%d" % stage], 1, T["q%d" % stage], T["s%d" % stage]
 
     def selections():
         g.vector.wait_ge(sem.sl, 1)
@@ -119,24 +122,26 @@ def rank_program(g, core, T, topo):
             g.vector.quantize_mx(T.w[:, 128 * b:128 * b + 128], T.ws[:, 128 * b:128 * b + 128],
                                  T.sel[:, 3 - b:515 - b]).then_inc(sem.cq, 1)
 
-    if rank is not None or any(len(terms) > 1 for terms, d, _ in SEND[me]):
+    sums = []
+    for terms, d, _ in SEND[me]:
+        if len(terms) > 1 and terms not in sums:
+            sums.append(terms)
+    if rank is not None or sums:
         g.vector.memset(T.ones[:], 1.0).then_inc(sem.one, 1)
         g.wait_ge(sem.one, 1)
         g.affine_select(T.sel[:], T.ones[:], [[-1, 516]], AluOpType.is_equal, 0.0, 3, 4).then_inc(sem.sl, 1)
 
     ready = {}
     if rank is not None:
-        def piece(i):
-            return slice(512 * i, 512 * i + 512)
-        g.sync.dma_start(T.b_sb[:], T.b[:]).then_inc(sem.ldb, 16)
-        for i, q in ((0, g.scalar), (1, g.sync), (2, g.scalar), (3, g.sync)):
-            q.dma_start(T.a_sb[:, piece(i)], T.a[:, piece(i)]).then_inc(sem["ld%d" % i], 16)
+        g.sync.dma_start(T.a_sb[:, 0:1536], T.a[:, 0:1536]).then_inc(sem.lda, 16)
+        g.scalar.dma_start(T.b_sb[:], T.b[:]).then_inc(sem.ldb, 16)
+        g.sync.dma_start(T.a_sb[:, 1536:2048], T.a[:, 1536:2048]).then_inc(sem.ldz, 16)
         g.vector.wait_ge(sem.ldb, 16)
         g.vector.quantize_mx(T.bq[:], T.bqs[:], T.b_sb[:]).then_inc(sem.qb, 1)
         for i in range(4):
-            g.vector.wait_ge(sem["ld%d" % i], 16)
+            g.vector.wait_ge(sem.lda if i < 3 else sem.ldz, 16)
             g.vector.quantize_mx(T.aq[:, 128 * i:128 * i + 128], T.aqs[:, 128 * i:128 * i + 128],
-                                 T.a_sb[:, piece(i)]).then_inc(sem["qa%d" % i], 1)
+                                 T.a_sb[:, 512 * i:512 * i + 512]).then_inc(sem["qa%d" % i], 1)
         g.tensor.wait_ge(sem.qb, 1)
 
         def product(ps, i, stop):
@@ -146,26 +151,31 @@ def rank_program(g, core, T, topo):
             g.tensor.wait_ge(sem["qa%d" % i], 1)
             product(T.p0, i, True).then_inc(sem["pe0_%d" % i], 1)
         empty(T.p0, T.h0, 0, (3,), (0, 1, 2))
-        pack(0)
-        ready[(rank,)] = (sem.qz0, 1, T.q0, T.s0)
+        ready[(rank,)] = pack(0)
         selections()
         for i in range(4):
             product(T.p1, i, False)
+        for terms in sums:
+            g.tensor.wait_ge(sem.cp0, 4)
+            for i in range(4):
+                product(T.p0, i, False)
+            g.tensor.wait_ge(sem.cq, 4)
+            for n, r in enumerate(terms[1:]):
+                unpack(T.p0, slot_of[(r,)], False, n == len(terms) - 2, 1)
+            empty(T.p0, T.h1, 1, (0, 1), (2, 3))
+            ready[terms] = pack(1)
         g.tensor.wait_ge(sem.cq, 4)
         for n, terms in enumerate(FINAL[rank]):
-            unpack(T.p1, slot_of[terms], False, n == len(FINAL[rank]) - 1, 1)
-        empty(T.p1, T.y_sb, 1, (0, 1), (2, 3))
-        g.sync.wait_ge(sem.cp1, 4)
+            unpack(T.p1, slot_of[terms], False, n == len(FINAL[rank]) - 1, 2)
+        empty(T.p1, T.y_sb, 2, (0, 1), (2, 3))
+        g.sync.wait_ge(sem.cp2, 4)
         g.sync.dma_start(T.y[:], T.y_sb[:]).then_inc(sem.stored, 16)
         g.sync.wait_ge(sem.stored, 16)
     else:
-        sums = []
         for terms, d, _ in SEND[me]:
             if len(terms) == 1:
                 k = slot_of[terms]
                 ready[terms] = (sem["arr%d" % k], 16) + landed(k)
-            elif terms not in sums:
-                sums.append(terms)
         if sums:
             selections()
             g.tensor.wait_ge(sem.cq, 4)
@@ -174,8 +184,7 @@ def rank_program(g, core, T, topo):
             for n, r in enumerate(terms):
                 unpack(ps, slot_of[(r,)], n == 0, n == len(terms) - 1, stage)
             empty(ps, T["h%d" % stage], stage, (0, 1), (2, 3))
-            pack(stage)
-            ready[terms] = (sem["qz%d" % stage], 1, T["q%d" % stage], T["s%d" % stage])
+            ready[terms] = pack(stage)
 
     away = next(c for c in range(WORLD) if (topo.host(c), topo.chip(c)) != (topo.host(core), topo.chip(core))
                 and topo.may_write(core, c))

from concourse.mybir import dt, AluOpType, ActivationFunctionType

BF, F8, U8, F32 = "bfloat16", "float8_e4m3fn_x4", "uint8", "float32"
SCRATCH = {
    "a_sb": ("sbuf", [128, 2048], BF), "b_sb": ("sbuf", [128, 512], BF),
    "aq": ("sbuf", [128, 512], F8), "aqs": ("sbuf", [128, 512], U8),
    "bq": ("sbuf", [128, 128], F8), "bqs": ("sbuf", [128, 128], U8),
    "ones": ("sbuf", [128, 516], BF), "sel": ("sbuf", [128, 516], BF),
    "w": ("sbuf", [128, 512], F8), "ws": ("sbuf", [128, 512], U8),
    "h0": ("sbuf", [128, 512], BF), "q0": ("sbuf", [128, 128], F8), "s0": ("sbuf", [128, 128], U8),
    "h1": ("sbuf", [128, 512], BF), "q1": ("sbuf", [128, 128], F8), "s1": ("sbuf", [128, 128], U8),
    "l0": ("sbuf", [128, 128], F8), "m0": ("sbuf", [128, 128], U8),
    "l1": ("sbuf", [128, 128], F8), "m1": ("sbuf", [128, 128], U8),
    "l2": ("sbuf", [128, 128], F8), "m2": ("sbuf", [128, 128], U8),
    "y_sb": ("sbuf", [128, 512], F32),
    "p0": ("psum", [128, 2048], F32), "p1": ("psum", [128, 2048], F32),
}
SEMAPHORES = (["ldb", "lda", "ldz", "qb", "qa0", "qa1", "qa2", "qa3", "one", "sl", "cq",
               "cp0", "cp1", "cp2", "qz0", "qz1", "arr0", "arr1", "arr2", "sent", "stored"]
              + ["pe%d_%d" % (s, b) for s in range(3) for b in range(4)])

OWN, MATE, NEAR, FAR = 0, 1, 0, 1
RELAYS = {
    "A": (0, OWN, NEAR), "B": (1, OWN, NEAR), "C": (1, OWN, FAR), "D": (2, OWN, FAR), "E": (2, OWN, NEAR),
    "F": (2, MATE, NEAR), "G": (3, OWN, NEAR), "H": (4, OWN, NEAR), "I": (5, OWN, NEAR), "J": (5, OWN, NEAR),
    "K": (5, MATE, NEAR), "L": (6, OWN, NEAR), "M": (0, MATE, FAR),
}
SEND = {
    0: [((0,), "D", 0), ((0,), "E", 0), ((0,), 2, 0)],
    1: [((1,), "C", 0), ((1,), "F", 0), ((1,), 3, 0), ((1,), "B", 1)],
    2: [((2,), "K", 0), ((2,), "E", 1), ((2,), "H", 0), ((2, 0), 4, 0)],
    3: [((3,), "I", 0), ((3,), "G", 1), ((3,), "J", 0), ((3, 1), 5, 0)],
    4: [((4,), "H", 1), ((4,), "L", 0), ((4,), "D", 0)],
    5: [((5,), "I", 0), ((5,), "G", 0), ((5,), "F", 0)],
    6: [((6,), "H", 0), ((6,), "A", 0), ((6,), "L", 1), ((6,), "K", 0)],
    7: [((7,), "B", 0), ((7,), "M", 0), ((7,), "C", 0)],
    8: [((8,), "E", 0), ((8,), "B", 0), ((8,), "A", 0)],
    9: [((9,), "A", 0), ((9,), "J", 0)],
    "A": [((9,), 2, 0), ((9, 6, 8), 0, 1), ((9, 6, 8), 1, 0)],
    "B": [((7,), 1, 0), ((7, 8), 9, 0), ((7, 8, 1), 2, 0)],
    "C": [((1,), 6, 0), ((7,), 0, 0)],
    "D": [((0,), 1, 0), ((0, 4), 5, 0)],
    "E": [((8, 2, 0), 3, 0)],
    "F": [((1,), 4, 0), ((5,), 0, 0)],
    "G": [((3, 5), 8, 0)],
    "H": [((4,), 7, 0), ((4, 6), 8, 0), ((4, 2), 6, 0)],
    "I": [((5,), 9, 0), ((5, 3), 6, 0), ((5, 3), 7, 0)],
    "J": [((9,), 3, 0), ((9, 3), 4, 0)],
    "K": [((2,), 5, 0), ((2, 6), 7, 0)],
    "L": [((6, 4), 9, 0)],
    "M": [((7,), 8, 0)],
}
FINAL = {
    0: [(9, 6, 8), (7,), (5,)], 1: [(7,), (0,), (9, 6, 8)], 2: [(0,), (9,), (7, 8, 1)], 3: [(1,), (9,), (8, 2, 0)],
    4: [(1,), (2, 0), (9, 3)], 5: [(2,), (3, 1), (0, 4)], 6: [(1,), (5, 3), (4, 2)], 7: [(4,), (5, 3), (2, 6)],
    8: [(4, 6), (3, 5), (7,)], 9: [(5,), (7, 8), (6, 4)],
}
WORLD = 512
PLACES = {}


def place(T, topo):
    if PLACES:
        return PLACES
    PLACES.update({r: c for r, c in enumerate(T.cores)})
    for name in sorted(RELAYS):
        anchor, mate, far = RELAYS[name]
        a = T.cores[anchor]
        for c in range(WORLD):
            here = topo.mates(c, a) if mate else (topo.host(c), topo.chip(c)) == (topo.host(a), topo.chip(a))
            if not here or (topo.die(c) != topo.die(a)) != bool(far) or c in PLACES.values():
                continue
            if any(topo.mates(c, d) and topo.may_write(c, d) for d in range(WORLD)):
                PLACES[name] = c
                break
    return PLACES


def rank_program(g, core, T, topo):
    at = place(T, topo)
    names = [n for n in at if at[n] == core]
    if not names:
        return
    me = names[0]
    rank = T.rank_of(core)
    sem = T.sem
    slots = {n: [] for n in at}
    for n in SEND:
        for terms, d, _ in SEND[n]:
            slots[d].append((n, terms))
    slot_of = {terms: k for k, (n, terms) in enumerate(slots[me])}

    def landed(k):
        return T["l%d" % k], T["m%d" % k]

    def unpack(ps, k, start, stop, stage):
        codes, plane = landed(k)
        g.tensor.wait_ge(sem["arr%d" % k], 16)
        for b in (0, 2, 1, 3):
            i = g.tensor.matmul_mx(ps[:, 512 * b:512 * b + 128], T.w[:, 128 * b:128 * b + 128],
                                   T.ws[:, 128 * b:128 * b + 128], codes[:], plane[:], start, stop)
            if stop:
                i.then_inc(sem["pe%d_%d" % (stage, b)], 1)

    def empty(ps, out, stage, vec, act):
        for b in vec:
            g.vector.wait_ge(sem["pe%d_%d" % (stage, b)], 1)
            g.vector.tensor_copy(out[:, b:512:4], ps[:, 512 * b:512 * b + 128]).then_inc(sem["cp%d" % stage], 1)
        for b in act:
            g.scalar.wait_ge(sem["pe%d_%d" % (stage, b)], 1)
            g.scalar.activation(out[:, b:512:4], ps[:, 512 * b:512 * b + 128],
                                ActivationFunctionType.Copy).then_inc(sem["cp%d" % stage], 1)

    def pack(stage):
        g.vector.wait_ge(sem["cp%d" % stage], 4)
        g.vector.quantize_mx(T["q%d" % stage][:], T["s%d" % stage][:], T["h%d" % stage][:]).then_inc(sem["qz%d" % stage], 1)
        return sem["qz%d" % stage], 1, T["q%d" % stage], T["s%d" % stage]

    def selections():
        g.vector.wait_ge(sem.sl, 1)
        for b in range(4):
            g.vector.quantize_mx(T.w[:, 128 * b:128 * b + 128], T.ws[:, 128 * b:128 * b + 128],
                                 T.sel[:, 3 - b:515 - b]).then_inc(sem.cq, 1)

    sums = []
    for terms, d, _ in SEND[me]:
        if len(terms) > 1 and terms not in sums:
            sums.append(terms)
    if rank is not None or sums:
        g.vector.memset(T.ones[:], 1.0).then_inc(sem.one, 1)
        g.wait_ge(sem.one, 1)
        g.affine_select(T.sel[:], T.ones[:], [[-1, 516]], AluOpType.is_equal, 0.0, 3, 4).then_inc(sem.sl, 1)

    ready = {}
    if rank is not None:
        g.sync.dma_start(T.a_sb[:, 0:1536], T.a[:, 0:1536]).then_inc(sem.lda, 16)
        g.scalar.dma_start(T.b_sb[:], T.b[:]).then_inc(sem.ldb, 16)
        g.sync.dma_start(T.a_sb[:, 1536:2048], T.a[:, 1536:2048]).then_inc(sem.ldz, 16)
        g.vector.wait_ge(sem.ldb, 16)
        g.vector.quantize_mx(T.bq[:], T.bqs[:], T.b_sb[:]).then_inc(sem.qb, 1)
        for i in range(4):
            g.vector.wait_ge(sem.lda if i < 3 else sem.ldz, 16)
            g.vector.quantize_mx(T.aq[:, 128 * i:128 * i + 128], T.aqs[:, 128 * i:128 * i + 128],
                                 T.a_sb[:, 512 * i:512 * i + 512]).then_inc(sem["qa%d" % i], 1)
        g.tensor.wait_ge(sem.qb, 1)

        def product(ps, i, stop):
            return g.tensor.matmul_mx(ps[:, 512 * i:512 * i + 128], T.aq[:, 128 * i:128 * i + 128],
                                      T.aqs[:, 128 * i:128 * i + 128], T.bq[:], T.bqs[:], True, stop)
        for i in range(4):
            g.tensor.wait_ge(sem["qa%d" % i], 1)
            product(T.p0, i, True).then_inc(sem["pe0_%d" % i], 1)
        empty(T.p0, T.h0, 0, (3,), (0, 1, 2))
        ready[(rank,)] = pack(0)
        selections()
        for i in range(4):
            product(T.p1, i, False)
        for terms in sums:
            g.tensor.wait_ge(sem.cp0, 4)
            for i in range(4):
                product(T.p0, i, False)
            g.tensor.wait_ge(sem.cq, 4)
            for n, r in enumerate(terms[1:]):
                unpack(T.p0, slot_of[(r,)], False, n == len(terms) - 2, 1)
            empty(T.p0, T.h1, 1, (0, 1), (2, 3))
            ready[terms] = pack(1)
        g.tensor.wait_ge(sem.cq, 4)
        for n, terms in enumerate(FINAL[rank]):
            unpack(T.p1, slot_of[terms], False, n == len(FINAL[rank]) - 1, 2)
        empty(T.p1, T.y_sb, 2, (0, 1), (2, 3))
        g.sync.wait_ge(sem.cp2, 4)
        g.sync.dma_start(T.y[:], T.y_sb[:]).then_inc(sem.stored, 16)
        g.sync.wait_ge(sem.stored, 16)
    else:
        for terms, d, _ in SEND[me]:
            if len(terms) == 1:
                k = slot_of[terms]
                ready[terms] = (sem["arr%d" % k], 16) + landed(k)
        if sums:
            selections()
            g.tensor.wait_ge(sem.cq, 4)
        for stage, terms in enumerate(sums):
            ps = T["p%d" % stage]
            for n, r in enumerate(terms):
                unpack(ps, slot_of[(r,)], n == 0, n == len(terms) - 1, stage)
            empty(ps, T["h%d" % stage], stage, (0, 1), (2, 3))
            ready[terms] = pack(stage)

    away = next(c for c in range(WORLD) if (topo.host(c), topo.chip(c)) != (topo.host(core), topo.chip(core))
                and topo.may_write(core, c))
    off = topo.mask(core, away)
    signals = 0
    for terms, d, beside in SEND[me]:
        s, v, codes, plane = ready[terms]
        g.wait_ge(s, v)
        dst = at[d]
        k = slots[d].index((me, terms))
        rid, pid = topo.addr(dst, core)
        mask = topo.mask(core, dst) & (~off if beside else off)
        cl, pl = landed(k)
        g.remote_dma(cl[:].bitcast(dt.uint8), codes[:].bitcast(dt.uint8), sem["arr%d" % k], sem.sent, pid, rid, mask)
        g.remote_dma(pl[:], plane[:], sem["arr%d" % k], sem.sent, pid, rid, mask)
        signals += 2 * bin(mask).count("1")
    g.wait_ge(sem.sent, signals)
